import numpy as np
import ml_dtypes


def mxq(x, axis, fmt="e4m3"):
    dtype, down = {"e4m3": (ml_dtypes.float8_e4m3fn, 7), "e5m2": (ml_dtypes.float8_e5m2, 14)}[fmt]
    v = np.moveaxis(np.asarray(x, np.float32).astype(ml_dtypes.bfloat16).astype(np.float64), axis, -1)
    blocks = v.reshape(v.shape[:-1] + (-1, 32))
    amax = np.abs(blocks).max(-1, keepdims=True)
    byte = np.maximum(np.where(amax > 0, np.frexp(amax)[1] - 1 + 127, 0) - down, 1)
    scale = np.exp2(byte - 127.0)
    codes = (blocks / scale).astype(np.float32).astype(dtype).astype(np.float64)
    return np.moveaxis((codes * scale).reshape(v.shape), -1, axis)


WIDE = False


def mx_kscale(k):
    if not WIDE:
        return np.ones(k)
    levels = np.array([10, -10, 5, -5, 0])
    if k % 512:
        return np.exp2(np.random.permutation(np.resize(levels, k // 32))).repeat(32)
    a = np.empty((k // 512, 16))
    for p in range(k // 512):
        a[p, :8] = np.random.permutation(np.resize(levels, 8))
        for g in range(8):
            far = levels[np.abs(levels - a[p, g]) >= 10]
            a[p, g + 8] = far[np.random.randint(len(far))]
    return np.exp2(a.ravel()).repeat(32)


def f64(x):
    return np.asarray(x).astype(np.float64)


def striped(idx):
    return np.tile(idx.reshape(-1, 16).T, (8, 1)).astype(np.uint16)


def unstriped(offs):
    return offs[:16].T.reshape(-1).astype(np.int64)


def striped8(idx):
    return np.concatenate([x.reshape(-1, 16).T for x in idx]).astype(np.uint16)


def runs(offs, k):
    lists = np.stack([offs[16 * r : 16 * r + 16].T.reshape(-1) for r in range(8)]).astype(np.int64)
    return lists[np.arange(k) % 512 // 64]


def pack_weight(w):
    k, n = w.shape
    w = f64(np.asarray(w, np.float32).astype(ml_dtypes.bfloat16)).reshape(k // 32, 32, n)
    amax = np.abs(w).max(1)
    byte = np.clip(np.where(amax > 0, np.frexp(amax)[1] - 1 + 127 - 7, 1), 1, 254)
    scaled = (w * np.exp2(127.0 - byte)[:, None, :]).reshape(k, n).astype(np.float32)
    words = np.ascontiguousarray(scaled.reshape(k // 512, 128, 4, n).transpose(0, 1, 3, 2)).astype(ml_dtypes.float8_e4m3fn).view(np.uint8)
    return words, np.ascontiguousarray(byte.astype(np.uint8).reshape(k // 512, 16, n))


def unpack_weight(words, scales):
    g, p, n, _ = words.shape
    vals = np.ascontiguousarray(words).view(ml_dtypes.float8_e4m3fn).astype(np.float64) * np.repeat(np.exp2(scales.astype(np.float64) - 127.0), 8, axis=1)[..., None]
    return vals.transpose(0, 1, 3, 2).reshape(g * 512, n)


def relu(v):
    return np.maximum(v, 0.0)


K, T, S, G, H, C, U = 512, 1024, 512, 2048, 512, 512, 1024


def setup_inputs():
    n = np.random.standard_normal
    s = mx_kscale(K)[:, None]
    packed_xT = pack_weight(n((K, T)) * s)
    packed_dT = pack_weight(n((K, G)) / s)
    return {
        "x_words": packed_xT[0],
        "x_scales": packed_xT[1],
        "d_words": packed_dT[0],
        "d_scales": packed_dT[1],
        "gs": (np.random.uniform(0.5, 1.5, (K, 1)) / s).astype(np.float32),
        "offs": striped(np.random.permutation(T)[:S]),
        "k1": striped8(np.random.randint(0, G, (8, H))),
        "n1": striped8(np.stack([np.random.permutation(S) for _ in range(8)])),
        "n2": striped8(np.stack([np.random.permutation(S) for _ in range(8)])),
        "cand": striped(np.random.permutation(T)[:C]),
        "n3": striped8(np.stack([np.random.permutation(U)[:S] for _ in range(8)])),
        "n4": striped8(np.stack([np.random.permutation(S) for _ in range(8)])),
    }


def reference(x_words, x_scales, d_words, d_scales, gs, offs, k1, n1, n2, cand, n3, n4):
    x_cand = unpack_weight(x_words, x_scales)[:, unstriped(cand)]
    d_k1 = unpack_weight(d_words, d_scales)[np.arange(K)[:, None], runs(k1, K)]
    xq = unpack_weight(x_words, x_scales)[:, unstriped(offs)]
    h = 0.0625 * (d_k1.T @ xq)
    z = f64(gs) * (np.minimum(np.maximum(h, h[np.arange(H)[:, None], runs(n1, H)]), h[np.arange(H)[:, None], runs(n2, H)]))
    s = 0.0625 * ((x_cand.T @ mxq(z, 0, "e4m3")))
    nw = s - (relu(s[np.arange(C)[:, None], runs(n4, C)]))
    out = np.zeros((C, U))
    out[np.arange(C)[:, None], runs(n3, C)] = nw
    return out

@@ -1,0 +1,238 @@
+from contextlib import ExitStack
+
+import concourse.mybir as mybir
+
+K, T, S, G, H, C, U = 512, 1024, 512, 2048, 512, 512, 1024
+FLOPS = 2 * K * H * S + 2 * K * C * S
+
+F32 = mybir.dt.float32
+BF16 = mybir.dt.bfloat16
+I32 = mybir.dt.int32
+U32 = mybir.dt.uint32
+U16 = mybir.dt.uint16
+U8 = mybir.dt.uint8
+FP8X4 = mybir.dt.float8_e4m3fn_x4
+ALU = mybir.AluOpType
+ACT = mybir.ActivationFunctionType
+
+P = 128
+PACK = 4
+SIXTEENTH = 0.0625
+HALVES = ((0, 256), (256, 512))
+CHUNKS = ((0, 256), (256, 384), (384, 512))
+VECTOR_N2 = ((0, 2), (0, 3))
+
+
+def entries(offsets, lo, hi):
+    return offsets[:, lo // 16 : hi // 16]
+
+
+def tile_picked_pqcminmxpagez_none_p_kernel(
+    tc, x_words, x_scales, d_words, d_scales, gs, offs, k1, n1, n2, cand, n3, n4, out
+):
+    nc = tc.nc
+    with ExitStack() as ctx:
+        keep = ctx.enter_context(tc.tile_pool(name="keep", bufs=1))
+        psum = ctx.enter_context(tc.psum_pool(name="psum", bufs=1))
+
+        def sb(name, shape, dtype, tag=None):
+            return keep.tile(shape, dtype, name=name, tag=tag or name, align_bytes=64)
+
+        def load_list(name, src):
+            tile = sb(name, [P, 32], U16)
+            nc.sync.dma_start(tile[:], src)
+            return tile
+
+        d_sc_table = sb("d_sc_table", [P, G], U8)
+        x_sc_table = sb("x_sc_table", [P, T], U8)
+        d_plane = sb("d_plane", [P, H], U8)
+        nc.vector.memset(d_sc_table[:].bitcast(I32), 0)
+        nc.vector.memset(x_sc_table[:].bitcast(I32), 0)
+        nc.vector.memset(d_plane[:].bitcast(I32), 0)
+
+        k1_t = load_list("k1_t", k1)
+        offs_t = load_list("offs_t", offs)
+        nc.scalar.dma_start(d_sc_table[0:P:8, :].bitcast(I32), d_scales[0].bitcast(I32))
+        d_table = sb("d_table", [P, G], U32)
+        nc.sync.dma_start(d_table[:].bitcast(I32), d_words[0].rearrange("p n t -> p (n t)").bitcast(I32))
+        x_table = sb("x_table", [P, T], U32)
+        nc.sync.dma_start(x_table[:].bitcast(I32), x_words[0].rearrange("p n t -> p (n t)").bitcast(I32))
+        for q in range(4):
+            nc.scalar.dma_start(
+                x_sc_table[32 * q : 32 * q + 4, :].bitcast(I32), x_scales[0, 4 * q : 4 * q + 4, :].bitcast(I32)
+            )
+        cand_t = load_list("cand_t", cand)
+        n1_t = load_list("n1_t", n1)
+        n2_t = load_list("n2_t", n2)
+        gain = sb("gain", [P, PACK], F32)
+        nc.gpsimd.dma_start(gain[:], gs.rearrange("(p t) o -> p (t o)", t=PACK))
+        n4_t = load_list("n4_t", n4)
+        n3_t = load_list("n3_t", n3)
+
+        pages = [sb(f"page{t}", [P, U], F32) for t in range(PACK)]
+        nc.vector.memset(pages[0][:], 0.0)
+        nc.vector.memset(pages[1][:], 0.0)
+        nc.scalar.copy(pages[2][:], pages[0][:])
+        nc.scalar.copy(pages[3][:], pages[0][:])
+
+        gain_size = sb("gain_size", [P, PACK], F32)
+        gain_sign = sb("gain_sign", [P, 256, PACK], BF16)
+        nc.scalar.activation(gain_size[:], gain[:], ACT.Abs, scale=SIXTEENTH)
+        nc.scalar.activation(gain_sign[:], gain[:].unsqueeze(1).to_broadcast([P, 256, PACK]), ACT.Sign)
+
+        d_sc_picked = sb("d_sc_picked", [P, H], U8)
+        d_sc_dealt = sb("d_sc_dealt", [P, H], U8)
+        xq_plane = sb("xq_plane", [P, S], U8)
+        d_picked = sb("d_picked", [P, H], U32)
+        d_codes = sb("d_codes", [P, H], U32)
+        nc.vector.tensor_copy(d_sc_picked[:], d_sc_table[:].indirect(k1_t[:]))
+        nc.vector.tensor_copy(xq_plane[:, 0:256], x_sc_table[:].indirect(entries(offs_t, 0, 256)))
+        nc.vector.tensor_copy(
+            d_sc_dealt[:].rearrange("p (t m) -> p m t", t=PACK), d_sc_picked[:].rearrange("p (m t) -> p m t", t=PACK)
+        )
+        for q in range(4):
+            nc.scalar.dma_start(
+                d_plane[32 * q : 32 * q + 4, :].bitcast(I32), d_sc_dealt[32 * q : 32 * q + 32 : 8, :].bitcast(I32)
+            )
+        nc.vector.tensor_copy(d_picked[:], d_table[:].indirect(k1_t[:]))
+        nc.vector.tensor_copy(xq_plane[:, 256:512], x_sc_table[:].indirect(entries(offs_t, 256, 512)))
+        nc.vector.tensor_copy(
+            d_codes[:].rearrange("p (t m) -> p m t", t=PACK), d_picked[:].rearrange("p (m t) -> p m t", t=PACK)
+        )
+
+        h = [sb(f"h{t}", [P, S], F32) for t in range(PACK)]
+        for half, (lo, hi) in enumerate(HALVES):
+            xq_codes = sb(f"xq_codes{half}", [P, hi - lo], U32)
+            nc.vector.tensor_copy(xq_codes[:], x_table[:].indirect(entries(offs_t, lo, hi)))
+            for pair in range(2):
+                bank = psum.tile([P, 2, hi - lo], F32, name=f"h_bank{half}{pair}", tag=f"h_bank{half}{pair}")
+                for u in range(2):
+                    t = 2 * pair + u
+                    nc.tensor.matmul_mx(
+                        out=bank[:, u, :],
+                        lhsT=d_codes[:, P * t : P * (t + 1)].bitcast(FP8X4),
+                        lhsT_scale=d_plane[:, P * t : P * (t + 1)],
+                        rhs=xq_codes[:].bitcast(FP8X4),
+                        rhs_scale=xq_plane[:, lo:hi],
+                        start=True,
+                        stop=True,
+                    )
+                for u in range(2):
+                    t = 2 * pair + u
+                    nc.scalar.activation(h[t][:, lo:hi], bank[:, u, :], ACT.Copy, scale=gain_size[:, t : t + 1])
+
+        c_codes = sb("c_codes", [P, C], U32)
+        c_plane = sb("c_plane", [P, C], U8)
+        nc.vector.tensor_copy(c_codes[:].rearrange("p (t m) -> p m t", t=PACK), x_table[:].indirect(cand_t[:]))
+        nc.vector.tensor_copy(c_plane[:].rearrange("p (t m) -> p m t", t=PACK), x_sc_table[:].indirect(cand_t[:]))
+
+        first = [sb(f"first{half}", [P, PACK, hi - lo], F32) for half, (lo, hi) in enumerate(HALVES)]
+        larger = [sb(f"larger{half}", [P, PACK, hi - lo], F32) for half, (lo, hi) in enumerate(HALVES)]
+        second = [sb(f"second{ci}", [P, PACK, hi - lo], F32) for ci, (lo, hi) in enumerate(CHUNKS)]
+        z_size = [sb(f"z_size{ci}", [P, hi - lo, PACK], BF16) for ci, (lo, hi) in enumerate(CHUNKS)]
+        z_full = [
+            sb(f"z_full{ci}", [P, hi - lo, PACK], BF16, tag="score_odd" if ci == 2 else None)
+            for ci, (lo, hi) in enumerate(CHUNKS)
+        ]
+        z_codes = [sb(f"z_codes{ci}", [P, hi - lo], U32) for ci, (lo, hi) in enumerate(CHUNKS)]
+        z_plane = [sb(f"z_plane{ci}", [P, hi - lo], U8) for ci, (lo, hi) in enumerate(CHUNKS)]
+        early_bank = psum.tile([P, 384], F32, name="early_bank")
+        last_bank = psum.tile([P, 128], F32, name="last_bank")
+        s_bank = [None] + [psum.tile([P, S], F32, name=f"s_bank{t}", tag=("s_bank1", "s_bank2", "h_bank00")[t - 1]) for t in range(1, PACK)]
+
+        def s_out(t, lo, hi):
+            if t > 0:
+                return s_bank[t][:, lo:hi]
+            return early_bank[:, lo:hi] if hi <= 384 else last_bank[:]
+
+        def fetch_first(half):
+            lo, hi = HALVES[half]
+            for t in range(PACK):
+                nc.scalar.activation(first[half][:, t, :], h[t][:].indirect(entries(n1_t, lo, hi)), ACT.Copy)
+
+        def fetch_second(ci):
+            lo, hi = CHUNKS[ci]
+            for t in range(PACK):
+                if (ci, t) in VECTOR_N2:
+                    nc.vector.tensor_copy(second[ci][:, t, :], h[t][:].indirect(entries(n2_t, lo, hi)))
+                else:
+                    nc.scalar.activation(second[ci][:, t, :], h[t][:].indirect(entries(n2_t, lo, hi)), ACT.Copy)
+
+        def take_larger(half, t):
+            lo, hi = HALVES[half]
+            nc.vector.tensor_tensor(larger[half][:, t, :], h[t][:, lo:hi], first[half][:, t, :], ALU.max)
+
+        def take_smaller(ci):
+            lo, hi = CHUNKS[ci]
+            half = lo // 256
+            a, b = lo - 256 * half, hi - 256 * half
+            nc.vector.tensor_tensor(
+                z_size[ci][:].rearrange("p (c i) t -> p c t i", i=4),
+                larger[half][:, :, a:b].rearrange("p t (c i) -> p c t i", i=4),
+                second[ci][:].rearrange("p t (c i) -> p c t i", i=4),
+                ALU.min,
+            )
+
+        def give_sign(ci):
+            lo, hi = CHUNKS[ci]
+            nc.vector.tensor_tensor(z_full[ci][:], z_size[ci][:], gain_sign[:, 0 : hi - lo, :], ALU.mult)
+
+        def score_chunk(ci):
+            lo, hi = CHUNKS[ci]
+            nc.vector.quantize_mx(
+                out=z_codes[ci][:].bitcast(FP8X4),
+                scales=z_plane[ci][:],
+                in_=z_full[ci][:].rearrange("p w t -> p (w t)"),
+            )
+            for t in range(PACK):
+                nc.tensor.matmul_mx(
+                    out=s_out(t, lo, hi),
+                    lhsT=c_codes[:, P * t : P * (t + 1)].bitcast(FP8X4),
+                    lhsT_scale=c_plane[:, P * t : P * (t + 1)],
+                    rhs=z_codes[ci][:].bitcast(FP8X4),
+                    rhs_scale=z_plane[ci][:],
+                    start=True,
+                    stop=True,
+                )
+
+        fetch_first(0)
+        fetch_second(0)
+        fetch_first(1)
+        fetch_second(1)
+        fetch_second(2)
+        for t in range(PACK):
+            take_larger(0, t)
+        take_smaller(0)
+        take_larger(1, 0)
+        give_sign(0)
+        take_larger(1, 1)
+        score_chunk(0)
+        take_larger(1, 2)
+        take_larger(1, 3)
+        take_smaller(1)
+        give_sign(1)
+        take_smaller(2)
+        score_chunk(1)
+        give_sign(2)
+        score_chunk(2)
+
+        out_rows = out.rearrange("(p t) w -> p t w", t=PACK)
+        for t in range(PACK):
+            score = sb(f"score{t}", [P, S], F32, tag=("score_even", "score_odd")[t % 2])
+            positive = sb(f"positive{t}", [P, S], F32, tag="positive")
+            pull = sb(f"pull{t}", [P, S], F32)
+            spans = ((0, 384), (384, S)) if t == 0 else ((0, S),)
+            for lo, hi in spans[:-1]:
+                nc.scalar.activation(positive[:, lo:hi], s_out(t, lo, hi), ACT.Relu, scale=SIXTEENTH)
+                nc.scalar.activation(score[:, lo:hi], s_out(t, lo, hi), ACT.Copy, scale=SIXTEENTH)
+            lo, hi = spans[-1]
+            nc.scalar.activation(positive[:, lo:hi], s_out(t, lo, hi), ACT.Relu, scale=SIXTEENTH)
+            nc.scalar.activation(pull[:, 0:256], positive[:].indirect(entries(n4_t, 0, 256)), ACT.Copy, scale=-1.0)
+            nc.scalar.activation(score[:, lo:hi], s_out(t, lo, hi), ACT.Copy, scale=SIXTEENTH)
+            nc.scalar.activation(pull[:, 256:S], positive[:].indirect(entries(n4_t, 256, S)), ACT.Copy, scale=-1.0)
+            pieces = HALVES if t == 0 else ((0, S),)
+            for lo, hi in pieces:
+                nc.vector.tensor_tensor(
+                    pages[t][:].indirect(entries(n3_t, lo, hi)), score[:, lo:hi], pull[:, lo:hi], ALU.add
+                )
+            nc.sync.dma_start(out_rows[:, t, :], pages[t][:])

@@ -20,7 +20,7 @@ PACK = 4
 SIXTEENTH = 0.0625
 HALVES = ((0, 256), (256, 512))
 CHUNKS = ((0, 256), (256, 384), (384, 512))
-VECTOR_N2 = ((0, 2), (0, 3))
+VECTOR_N2 = ((0, 0), (0, 1), (0, 2), (0, 3))
 
 
 def entries(offsets, lo, hi):
@@ -33,6 +33,7 @@ def tile_picked_pqcminmxpagez_none_p_kernel(
     nc = tc.nc
     with ExitStack() as ctx:
         keep = ctx.enter_context(tc.tile_pool(name="keep", bufs=1))
+        shared = ctx.enter_context(tc.tile_pool(name="shared", bufs=1))
         psum = ctx.enter_context(tc.psum_pool(name="psum", bufs=1))
 
         def sb(name, shape, dtype, tag=None):
@@ -52,57 +53,59 @@ def tile_picked_pqcminmxpagez_none_p_kernel(
 
         k1_t = load_list("k1_t", k1)
         offs_t = load_list("offs_t", offs)
-        nc.scalar.dma_start(d_sc_table[0:P:8, :].bitcast(I32), d_scales[0].bitcast(I32))
+        nc.sync.dma_start(d_sc_table[0:P:8, :].bitcast(I32), d_scales[0].bitcast(I32))
         d_table = sb("d_table", [P, G], U32)
         nc.sync.dma_start(d_table[:].bitcast(I32), d_words[0].rearrange("p n t -> p (n t)").bitcast(I32))
-        x_table = sb("x_table", [P, T], U32)
-        nc.sync.dma_start(x_table[:].bitcast(I32), x_words[0].rearrange("p n t -> p (n t)").bitcast(I32))
         for q in range(4):
-            nc.scalar.dma_start(
+            nc.sync.dma_start(
                 x_sc_table[32 * q : 32 * q + 4, :].bitcast(I32), x_scales[0, 4 * q : 4 * q + 4, :].bitcast(I32)
             )
-        cand_t = load_list("cand_t", cand)
-        n1_t = load_list("n1_t", n1)
-        n2_t = load_list("n2_t", n2)
+        x_table = sb("x_table", [P, T], U32)
+        nc.sync.dma_start(x_table[:].bitcast(I32), x_words[0].rearrange("p n t -> p (n t)").bitcast(I32))
         gain = sb("gain", [P, PACK], F32)
         nc.gpsimd.dma_start(gain[:], gs.rearrange("(p t) o -> p (t o)", t=PACK))
-        n4_t = load_list("n4_t", n4)
-        n3_t = load_list("n3_t", n3)
 
         pages = [sb(f"page{t}", [P, U], F32) for t in range(PACK)]
         nc.vector.memset(pages[0][:], 0.0)
-        nc.vector.memset(pages[1][:], 0.0)
-        nc.scalar.copy(pages[2][:], pages[0][:])
-        nc.scalar.copy(pages[3][:], pages[0][:])
+        for t in range(1, PACK):
+            nc.scalar.copy(pages[t][:], pages[0][:])
 
         gain_size = sb("gain_size", [P, PACK], F32)
         gain_sign = sb("gain_sign", [P, 256, PACK], BF16)
         nc.scalar.activation(gain_size[:], gain[:], ACT.Abs, scale=SIXTEENTH)
         nc.scalar.activation(gain_sign[:], gain[:].unsqueeze(1).to_broadcast([P, 256, PACK]), ACT.Sign)
 
-        d_sc_picked = sb("d_sc_picked", [P, H], U8)
+        d_sc_picked = shared.tile([P, H], U8, name="d_sc_picked", align_bytes=64, offset=4 * H - H // 2)
         d_sc_dealt = sb("d_sc_dealt", [P, H], U8)
-        xq_plane = sb("xq_plane", [P, S], U8)
-        d_picked = sb("d_picked", [P, H], U32)
+        xq_plane = shared.tile([P, S], U8, name="xq_plane", align_bytes=64, offset=4 * H)
+        d_picked = shared.tile([P, H], U32, name="d_picked", align_bytes=64, offset=0)
         d_codes = sb("d_codes", [P, H], U32)
         nc.vector.tensor_copy(d_sc_picked[:], d_sc_table[:].indirect(k1_t[:]))
-        nc.vector.tensor_copy(xq_plane[:, 0:256], x_sc_table[:].indirect(entries(offs_t, 0, 256)))
         nc.vector.tensor_copy(
-            d_sc_dealt[:].rearrange("p (t m) -> p m t", t=PACK), d_sc_picked[:].rearrange("p (m t) -> p m t", t=PACK)
+            d_sc_dealt[:].rearrange("p (t a i) -> p a t i", t=PACK, i=16),
+            d_sc_picked[:].rearrange("p (a i t) -> p a t i", t=PACK, i=16),
         )
         for q in range(4):
-            nc.scalar.dma_start(
+            nc.sync.dma_start(
                 d_plane[32 * q : 32 * q + 4, :].bitcast(I32), d_sc_dealt[32 * q : 32 * q + 32 : 8, :].bitcast(I32)
             )
+        cand_t = load_list("cand_t", cand)
+        n1_t = load_list("n1_t", n1)
+        n2_t = load_list("n2_t", n2)
+        n4_t = load_list("n4_t", n4)
+        n3_t = load_list("n3_t", n3)
         nc.vector.tensor_copy(d_picked[:], d_table[:].indirect(k1_t[:]))
-        nc.vector.tensor_copy(xq_plane[:, 256:512], x_sc_table[:].indirect(entries(offs_t, 256, 512)))
+        nc.vector.tensor_copy(xq_plane[:, 0:256], x_sc_table[:].indirect(entries(offs_t, 0, 256)))
         nc.vector.tensor_copy(
-            d_codes[:].rearrange("p (t m) -> p m t", t=PACK), d_picked[:].rearrange("p (m t) -> p m t", t=PACK)
+            d_codes[:].rearrange("p (t a i) -> p a t i", t=PACK, i=4),
+            d_picked[:].rearrange("p (a i t) -> p a t i", t=PACK, i=4),
         )
 
         h = [sb(f"h{t}", [P, S], F32) for t in range(PACK)]
         for half, (lo, hi) in enumerate(HALVES):
             xq_codes = sb(f"xq_codes{half}", [P, hi - lo], U32)
+            if half == 1:
+                nc.vector.tensor_copy(xq_plane[:, lo:hi], x_sc_table[:].indirect(entries(offs_t, lo, hi)))
             nc.vector.tensor_copy(xq_codes[:], x_table[:].indirect(entries(offs_t, lo, hi)))
             for pair in range(2):
                 bank = psum.tile([P, 2, hi - lo], F32, name=f"h_bank{half}{pair}", tag=f"h_bank{half}{pair}")
@@ -136,14 +139,16 @@ def tile_picked_pqcminmxpagez_none_p_kernel(
         ]
         z_codes = [sb(f"z_codes{ci}", [P, hi - lo], U32) for ci, (lo, hi) in enumerate(CHUNKS)]
         z_plane = [sb(f"z_plane{ci}", [P, hi - lo], U8) for ci, (lo, hi) in enumerate(CHUNKS)]
-        early_bank = psum.tile([P, 384], F32, name="early_bank")
-        last_bank = psum.tile([P, 128], F32, name="last_bank")
-        s_bank = [None] + [psum.tile([P, S], F32, name=f"s_bank{t}", tag=("s_bank1", "s_bank2", "h_bank00")[t - 1]) for t in range(1, PACK)]
+        lead_bank = [psum.tile([P, hi - lo], F32, name=f"lead_bank{ci}") for ci, (lo, hi) in enumerate(CHUNKS)]
+        s_bank = [None] + [
+            psum.tile([P, S], F32, name=f"s_bank{t}", tag=("s_bank1", "h_bank00", "h_bank01")[t - 1])
+            for t in range(1, PACK)
+        ]
 
         def s_out(t, lo, hi):
             if t > 0:
                 return s_bank[t][:, lo:hi]
-            return early_bank[:, lo:hi] if hi <= 384 else last_bank[:]
+            return lead_bank[CHUNKS.index((lo, hi))][:]
 
         def fetch_first(half):
             lo, hi = HALVES[half]
@@ -221,13 +226,19 @@ def tile_picked_pqcminmxpagez_none_p_kernel(
             score = sb(f"score{t}", [P, S], F32, tag=("score_even", "score_odd")[t % 2])
             positive = sb(f"positive{t}", [P, S], F32, tag="positive")
             pull = sb(f"pull{t}", [P, S], F32)
-            spans = ((0, 384), (384, S)) if t == 0 else ((0, S),)
+            spans = CHUNKS if t == 0 else ((0, S),)
             for lo, hi in spans[:-1]:
                 nc.scalar.activation(positive[:, lo:hi], s_out(t, lo, hi), ACT.Relu, scale=SIXTEENTH)
                 nc.scalar.activation(score[:, lo:hi], s_out(t, lo, hi), ACT.Copy, scale=SIXTEENTH)
             lo, hi = spans[-1]
             nc.scalar.activation(positive[:, lo:hi], s_out(t, lo, hi), ACT.Relu, scale=SIXTEENTH)
-            nc.scalar.activation(pull[:, 0:256], positive[:].indirect(entries(n4_t, 0, 256)), ACT.Copy, scale=-1.0)
+            if t == 0:
+                nc.scalar.activation(pull[:, 0:128], positive[:].indirect(entries(n4_t, 0, 128)), ACT.Copy, scale=-1.0)
+                nc.vector.tensor_scalar(
+                    pull[:, 128:256], positive[:].indirect(entries(n4_t, 128, 256)), -1.0, 0.0, ALU.mult, ALU.add
+                )
+            else:
+                nc.scalar.activation(pull[:, 0:256], positive[:].indirect(entries(n4_t, 0, 256)), ACT.Copy, scale=-1.0)
             nc.scalar.activation(score[:, lo:hi], s_out(t, lo, hi), ACT.Copy, scale=SIXTEENTH)
             nc.scalar.activation(pull[:, 256:S], positive[:].indirect(entries(n4_t, 256, S)), ACT.Copy, scale=-1.0)
             pieces = HALVES if t == 0 else ((0, S),)

@@ -17,14 +17,18 @@ ACT = mybir.ActivationFunctionType
 
 P = 128
 PACK = 4
+GROUP = 16
 SIXTEENTH = 0.0625
-HALVES = ((0, 256), (256, 512))
-CHUNKS = ((0, 256), (256, 384), (384, 512))
-VECTOR_N2 = ((0, 0), (0, 1), (0, 2), (0, 3))
+HALF, QUARTER = S // 2, S // 4
+
+HALVES = ((0, HALF), (HALF, S))
+CHUNKS = ((0, HALF), (HALF, HALF + QUARTER), (HALF + QUARTER, S))
+SPANS = ((0, 256), (256, 384), (384, 448), (448, 512))
+VECTOR_N2 = ((0, 0), (0, 1), (0, 2), (0, 3), (1, 0))
 
 
 def entries(offsets, lo, hi):
-    return offsets[:, lo // 16 : hi // 16]
+    return offsets[:, lo // GROUP : hi // GROUP]
 
 
 def tile_picked_pqcminmxpagez_none_p_kernel(
@@ -36,169 +40,182 @@ def tile_picked_pqcminmxpagez_none_p_kernel(
         shared = ctx.enter_context(tc.tile_pool(name="shared", bufs=1))
         psum = ctx.enter_context(tc.psum_pool(name="psum", bufs=1))
 
-        def sb(name, shape, dtype, tag=None):
+        def sbuf(name, shape, dtype, tag=None):
             return keep.tile(shape, dtype, name=name, tag=tag or name, align_bytes=64)
 
-        def load_list(name, src):
-            tile = sb(name, [P, 32], U16)
-            nc.sync.dma_start(tile[:], src)
+        def load_list(name, source):
+            tile = sbuf(name, [P, S // GROUP], U16)
+            nc.sync.dma_start(tile[:], source)
             return tile
 
-        d_sc_table = sb("d_sc_table", [P, G], U8)
-        x_sc_table = sb("x_sc_table", [P, T], U8)
-        d_plane = sb("d_plane", [P, H], U8)
-        nc.vector.memset(d_sc_table[:].bitcast(I32), 0)
-        nc.vector.memset(x_sc_table[:].bitcast(I32), 0)
+        d_byte_table = sbuf("d_byte_table", [P, G], U8)
+        x_byte_table = sbuf("x_byte_table", [P, T], U8)
+        d_plane = sbuf("d_plane", [P, H], U8)
+        nc.vector.memset(d_byte_table[:].bitcast(I32), 0)
+        nc.vector.memset(x_byte_table[:].bitcast(I32), 0)
         nc.vector.memset(d_plane[:].bitcast(I32), 0)
 
-        k1_t = load_list("k1_t", k1)
-        offs_t = load_list("offs_t", offs)
-        nc.sync.dma_start(d_sc_table[0:P:8, :].bitcast(I32), d_scales[0].bitcast(I32))
-        d_table = sb("d_table", [P, G], U32)
-        nc.sync.dma_start(d_table[:].bitcast(I32), d_words[0].rearrange("p n t -> p (n t)").bitcast(I32))
-        for q in range(4):
+        k1_list = load_list("k1_list", k1)
+        offs_list = load_list("offs_list", offs)
+        nc.sync.dma_start(d_byte_table[0:P:8, :].bitcast(I32), d_scales[0].bitcast(I32))
+        d_word_table = sbuf("d_word_table", [P, G], U32)
+        nc.sync.dma_start(d_word_table[:].bitcast(I32), d_words[0].rearrange("p n j -> p (n j)").bitcast(I32))
+        for q in range(PACK):
             nc.sync.dma_start(
-                x_sc_table[32 * q : 32 * q + 4, :].bitcast(I32), x_scales[0, 4 * q : 4 * q + 4, :].bitcast(I32)
+                x_byte_table[32 * q : 32 * q + 4, :].bitcast(I32), x_scales[0, 4 * q : 4 * q + 4, :].bitcast(I32)
             )
-        x_table = sb("x_table", [P, T], U32)
-        nc.sync.dma_start(x_table[:].bitcast(I32), x_words[0].rearrange("p n t -> p (n t)").bitcast(I32))
-        gain = sb("gain", [P, PACK], F32)
-        nc.gpsimd.dma_start(gain[:], gs.rearrange("(p t) o -> p (t o)", t=PACK))
+        x_word_table = sbuf("x_word_table", [P, T], U32)
+        nc.sync.dma_start(x_word_table[:].bitcast(I32), x_words[0].rearrange("p n j -> p (n j)").bitcast(I32))
+        gain = sbuf("gain", [P, PACK], F32)
+        nc.sync.dma_start(gain[:], gs.rearrange("(p t) o -> p (t o)", t=PACK))
 
-        pages = [sb(f"page{t}", [P, U], F32) for t in range(PACK)]
+        pages = [sbuf(f"page{t}", [P, U], F32) for t in range(PACK)]
         nc.vector.memset(pages[0][:], 0.0)
         for t in range(1, PACK):
             nc.scalar.copy(pages[t][:], pages[0][:])
 
-        gain_size = sb("gain_size", [P, PACK], F32)
-        gain_sign = sb("gain_sign", [P, 256, PACK], BF16)
+        gain_size = sbuf("gain_size", [P, PACK], F32)
+        gain_sign = sbuf("gain_sign", [P, HALF, PACK], BF16)
         nc.scalar.activation(gain_size[:], gain[:], ACT.Abs, scale=SIXTEENTH)
-        nc.scalar.activation(gain_sign[:], gain[:].unsqueeze(1).to_broadcast([P, 256, PACK]), ACT.Sign)
+        nc.scalar.activation(gain_sign[:], gain[:].unsqueeze(1).to_broadcast([P, HALF, PACK]), ACT.Sign)
 
-        d_sc_picked = shared.tile([P, H], U8, name="d_sc_picked", align_bytes=64, offset=4 * H - H // 2)
-        d_sc_dealt = sb("d_sc_dealt", [P, H], U8)
-        xq_plane = shared.tile([P, S], U8, name="xq_plane", align_bytes=64, offset=4 * H)
-        d_picked = shared.tile([P, H], U32, name="d_picked", align_bytes=64, offset=0)
-        d_codes = sb("d_codes", [P, H], U32)
-        nc.vector.tensor_copy(d_sc_picked[:], d_sc_table[:].indirect(k1_t[:]))
+        word_bytes = 4 * H
+        d_bytes_picked = shared.tile([P, H], U8, name="d_bytes_picked", align_bytes=64, offset=word_bytes - H // 2)
+        d_bytes_dealt = shared.tile([P, H], U8, name="d_bytes_dealt", align_bytes=64, offset=word_bytes + HALF)
+        token_plane = [
+            shared.tile([P, HALF], U8, name=f"token_plane{half}", align_bytes=64, offset=word_bytes + HALF * half)
+            for half in range(2)
+        ]
+        d_words_picked = shared.tile([P, H], U32, name="d_words_picked", align_bytes=64, offset=0)
+        d_codes = sbuf("d_codes", [P, H], U32)
+
+        nc.vector.tensor_copy(d_bytes_picked[:], d_byte_table[:].indirect(k1_list[:]))
         nc.vector.tensor_copy(
-            d_sc_dealt[:].rearrange("p (t a i) -> p a t i", t=PACK, i=16),
-            d_sc_picked[:].rearrange("p (a i t) -> p a t i", t=PACK, i=16),
+            d_bytes_dealt[:].rearrange("p (t a i) -> p a t i", t=PACK, i=16),
+            d_bytes_picked[:].rearrange("p (a i t) -> p a t i", t=PACK, i=16),
         )
-        for q in range(4):
+        for q in range(PACK):
             nc.sync.dma_start(
-                d_plane[32 * q : 32 * q + 4, :].bitcast(I32), d_sc_dealt[32 * q : 32 * q + 32 : 8, :].bitcast(I32)
+                d_plane[32 * q : 32 * q + 4, :].bitcast(I32), d_bytes_dealt[32 * q : 32 * q + 32 : 8, :].bitcast(I32)
             )
-        cand_t = load_list("cand_t", cand)
-        n1_t = load_list("n1_t", n1)
-        n2_t = load_list("n2_t", n2)
-        n4_t = load_list("n4_t", n4)
-        n3_t = load_list("n3_t", n3)
-        nc.vector.tensor_copy(d_picked[:], d_table[:].indirect(k1_t[:]))
-        nc.vector.tensor_copy(xq_plane[:, 0:256], x_sc_table[:].indirect(entries(offs_t, 0, 256)))
+        cand_list = load_list("cand_list", cand)
+        n1_list = load_list("n1_list", n1)
+        n2_list = load_list("n2_list", n2)
+        n4_list = load_list("n4_list", n4)
+        n3_list = load_list("n3_list", n3)
+        nc.vector.tensor_copy(d_words_picked[:], d_word_table[:].indirect(k1_list[:]))
+        nc.vector.tensor_copy(token_plane[0][:], x_byte_table[:].indirect(entries(offs_list, 0, HALF)))
         nc.vector.tensor_copy(
             d_codes[:].rearrange("p (t a i) -> p a t i", t=PACK, i=4),
-            d_picked[:].rearrange("p (a i t) -> p a t i", t=PACK, i=4),
+            d_words_picked[:].rearrange("p (a i t) -> p a t i", t=PACK, i=4),
         )
 
-        h = [sb(f"h{t}", [P, S], F32) for t in range(PACK)]
+        u = [sbuf(f"u{t}", [P, S], F32) for t in range(PACK)]
         for half, (lo, hi) in enumerate(HALVES):
-            xq_codes = sb(f"xq_codes{half}", [P, hi - lo], U32)
+            token_codes = sbuf(f"token_codes{half}", [P, hi - lo], U32)
             if half == 1:
-                nc.vector.tensor_copy(xq_plane[:, lo:hi], x_sc_table[:].indirect(entries(offs_t, lo, hi)))
-            nc.vector.tensor_copy(xq_codes[:], x_table[:].indirect(entries(offs_t, lo, hi)))
+                nc.vector.tensor_copy(token_plane[1][:], x_byte_table[:].indirect(entries(offs_list, lo, hi)))
+            nc.vector.tensor_copy(token_codes[:], x_word_table[:].indirect(entries(offs_list, lo, hi)))
             for pair in range(2):
                 bank = psum.tile([P, 2, hi - lo], F32, name=f"h_bank{half}{pair}", tag=f"h_bank{half}{pair}")
-                for u in range(2):
-                    t = 2 * pair + u
+                for slot in range(2):
+                    t = 2 * pair + slot
                     nc.tensor.matmul_mx(
-                        out=bank[:, u, :],
+                        out=bank[:, slot, :],
                         lhsT=d_codes[:, P * t : P * (t + 1)].bitcast(FP8X4),
                         lhsT_scale=d_plane[:, P * t : P * (t + 1)],
-                        rhs=xq_codes[:].bitcast(FP8X4),
-                        rhs_scale=xq_plane[:, lo:hi],
+                        rhs=token_codes[:].bitcast(FP8X4),
+                        rhs_scale=token_plane[half][:],
                         start=True,
                         stop=True,
                     )
-                for u in range(2):
-                    t = 2 * pair + u
-                    nc.scalar.activation(h[t][:, lo:hi], bank[:, u, :], ACT.Copy, scale=gain_size[:, t : t + 1])
+                for slot in range(2):
+                    t = 2 * pair + slot
+                    nc.scalar.activation(u[t][:, lo:hi], bank[:, slot, :], ACT.Copy, scale=gain_size[:, t : t + 1])
 
-        c_codes = sb("c_codes", [P, C], U32)
-        c_plane = sb("c_plane", [P, C], U8)
-        nc.vector.tensor_copy(c_codes[:].rearrange("p (t m) -> p m t", t=PACK), x_table[:].indirect(cand_t[:]))
-        nc.vector.tensor_copy(c_plane[:].rearrange("p (t m) -> p m t", t=PACK), x_sc_table[:].indirect(cand_t[:]))
+        cand_codes = sbuf("cand_codes", [P, C], U32)
+        cand_plane = sbuf("cand_plane", [P, C], U8)
+        nc.vector.tensor_copy(
+            cand_codes[:].rearrange("p (t m) -> p m t", t=PACK), x_word_table[:].indirect(cand_list[:])
+        )
+        nc.vector.tensor_copy(
+            cand_plane[:].rearrange("p (t m) -> p m t", t=PACK), x_byte_table[:].indirect(cand_list[:])
+        )
 
-        first = [sb(f"first{half}", [P, PACK, hi - lo], F32) for half, (lo, hi) in enumerate(HALVES)]
-        larger = [sb(f"larger{half}", [P, PACK, hi - lo], F32) for half, (lo, hi) in enumerate(HALVES)]
-        second = [sb(f"second{ci}", [P, PACK, hi - lo], F32) for ci, (lo, hi) in enumerate(CHUNKS)]
-        z_size = [sb(f"z_size{ci}", [P, hi - lo, PACK], BF16) for ci, (lo, hi) in enumerate(CHUNKS)]
-        z_full = [
-            sb(f"z_full{ci}", [P, hi - lo, PACK], BF16, tag="score_odd" if ci == 2 else None)
-            for ci, (lo, hi) in enumerate(CHUNKS)
+        first = [sbuf(f"first{half}", [P, PACK, hi - lo], F32) for half, (lo, hi) in enumerate(HALVES)]
+        larger = [sbuf(f"larger{half}", [P, PACK, hi - lo], F32) for half, (lo, hi) in enumerate(HALVES)]
+        second = [sbuf(f"second{chunk}", [P, PACK, hi - lo], F32) for chunk, (lo, hi) in enumerate(CHUNKS)]
+        z_unsigned = [sbuf(f"z_unsigned{span}", [P, hi - lo, PACK], BF16) for span, (lo, hi) in enumerate(SPANS)]
+        z = [
+            sbuf(f"z{span}", [P, hi - lo, PACK], BF16, tag="score_odd" if span == len(SPANS) - 1 else None)
+            for span, (lo, hi) in enumerate(SPANS)
         ]
-        z_codes = [sb(f"z_codes{ci}", [P, hi - lo], U32) for ci, (lo, hi) in enumerate(CHUNKS)]
-        z_plane = [sb(f"z_plane{ci}", [P, hi - lo], U8) for ci, (lo, hi) in enumerate(CHUNKS)]
-        lead_bank = [psum.tile([P, hi - lo], F32, name=f"lead_bank{ci}") for ci, (lo, hi) in enumerate(CHUNKS)]
-        s_bank = [None] + [
-            psum.tile([P, S], F32, name=f"s_bank{t}", tag=("s_bank1", "h_bank00", "h_bank01")[t - 1])
-            for t in range(1, PACK)
+        z_codes = sbuf("z_codes", [P, S], U32)
+        z_plane = sbuf("z_plane", [P, S], U8)
+        lead_tags = ("lead0", "lead1", "lead2", "h_bank10")
+        lead_bank = [
+            psum.tile([P, hi - lo], F32, name=f"lead_bank{span}", tag=lead_tags[span])
+            for span, (lo, hi) in enumerate(SPANS)
         ]
+        later_tags = {1: "s_bank1", 2: "h_bank00", 3: "h_bank01"}
+        later_bank = {t: psum.tile([P, S], F32, name=f"s_bank{t}", tag=later_tags[t]) for t in range(1, PACK)}
 
-        def s_out(t, lo, hi):
+        def s_sums(t, lo, hi):
             if t > 0:
-                return s_bank[t][:, lo:hi]
-            return lead_bank[CHUNKS.index((lo, hi))][:]
+                return later_bank[t][:, lo:hi]
+            return lead_bank[SPANS.index((lo, hi))][:]
 
         def fetch_first(half):
             lo, hi = HALVES[half]
             for t in range(PACK):
-                nc.scalar.activation(first[half][:, t, :], h[t][:].indirect(entries(n1_t, lo, hi)), ACT.Copy)
+                nc.scalar.activation(first[half][:, t, :], u[t][:].indirect(entries(n1_list, lo, hi)), ACT.Copy)
 
-        def fetch_second(ci):
-            lo, hi = CHUNKS[ci]
+        def fetch_second(chunk):
+            lo, hi = CHUNKS[chunk]
             for t in range(PACK):
-                if (ci, t) in VECTOR_N2:
-                    nc.vector.tensor_copy(second[ci][:, t, :], h[t][:].indirect(entries(n2_t, lo, hi)))
+                if (chunk, t) in VECTOR_N2:
+                    nc.vector.tensor_copy(second[chunk][:, t, :], u[t][:].indirect(entries(n2_list, lo, hi)))
                 else:
-                    nc.scalar.activation(second[ci][:, t, :], h[t][:].indirect(entries(n2_t, lo, hi)), ACT.Copy)
+                    nc.scalar.activation(second[chunk][:, t, :], u[t][:].indirect(entries(n2_list, lo, hi)), ACT.Copy)
 
         def take_larger(half, t):
             lo, hi = HALVES[half]
-            nc.vector.tensor_tensor(larger[half][:, t, :], h[t][:, lo:hi], first[half][:, t, :], ALU.max)
+            nc.vector.tensor_tensor(larger[half][:, t, :], u[t][:, lo:hi], first[half][:, t, :], ALU.max)
 
-        def take_smaller(ci):
-            lo, hi = CHUNKS[ci]
-            half = lo // 256
-            a, b = lo - 256 * half, hi - 256 * half
+        def take_smaller(span):
+            lo, hi = SPANS[span]
+            half, chunk = lo // HALF, min(span, len(CHUNKS) - 1)
+            half_lo, chunk_lo = HALVES[half][0], CHUNKS[chunk][0]
             nc.vector.tensor_tensor(
-                z_size[ci][:].rearrange("p (c i) t -> p c t i", i=4),
-                larger[half][:, :, a:b].rearrange("p t (c i) -> p c t i", i=4),
-                second[ci][:].rearrange("p t (c i) -> p c t i", i=4),
+                z_unsigned[span][:].rearrange("p (c i) t -> p c t i", i=4),
+                larger[half][:, :, lo - half_lo : hi - half_lo].rearrange("p t (c i) -> p c t i", i=4),
+                second[chunk][:, :, lo - chunk_lo : hi - chunk_lo].rearrange("p t (c i) -> p c t i", i=4),
                 ALU.min,
             )
 
-        def give_sign(ci):
-            lo, hi = CHUNKS[ci]
-            nc.vector.tensor_tensor(z_full[ci][:], z_size[ci][:], gain_sign[:, 0 : hi - lo, :], ALU.mult)
+        def give_sign(span):
+            lo, hi = SPANS[span]
+            nc.vector.tensor_tensor(z[span][:], z_unsigned[span][:], gain_sign[:, 0 : hi - lo, :], ALU.mult)
 
-        def score_chunk(ci):
-            lo, hi = CHUNKS[ci]
-            nc.vector.quantize_mx(
-                out=z_codes[ci][:].bitcast(FP8X4),
-                scales=z_plane[ci][:],
-                in_=z_full[ci][:].rearrange("p w t -> p (w t)"),
+        def multiply(t, lo, hi):
+            nc.tensor.matmul_mx(
+                out=s_sums(t, lo, hi),
+                lhsT=cand_codes[:, P * t : P * (t + 1)].bitcast(FP8X4),
+                lhsT_scale=cand_plane[:, P * t : P * (t + 1)],
+                rhs=z_codes[:, lo:hi].bitcast(FP8X4),
+                rhs_scale=z_plane[:, lo:hi],
+                start=True,
+                stop=True,
             )
-            for t in range(PACK):
-                nc.tensor.matmul_mx(
-                    out=s_out(t, lo, hi),
-                    lhsT=c_codes[:, P * t : P * (t + 1)].bitcast(FP8X4),
-                    lhsT_scale=c_plane[:, P * t : P * (t + 1)],
-                    rhs=z_codes[ci][:].bitcast(FP8X4),
-                    rhs_scale=z_plane[ci][:],
-                    start=True,
-                    stop=True,
-                )
+
+        def quantise(span):
+            lo, hi = SPANS[span]
+            nc.vector.quantize_mx(
+                out=z_codes[:, lo:hi].bitcast(FP8X4),
+                scales=z_plane[:, lo:hi],
+                in_=z[span][:].rearrange("p c t -> p (c t)"),
+            )
+            multiply(0, lo, hi)
 
         fetch_first(0)
         fetch_second(0)
@@ -207,43 +224,58 @@ def tile_picked_pqcminmxpagez_none_p_kernel(
         fetch_second(2)
         for t in range(PACK):
             take_larger(0, t)
-        take_smaller(0)
         take_larger(1, 0)
-        give_sign(0)
+        take_smaller(0)
         take_larger(1, 1)
-        score_chunk(0)
+        give_sign(0)
         take_larger(1, 2)
+        quantise(0)
         take_larger(1, 3)
         take_smaller(1)
         give_sign(1)
         take_smaller(2)
-        score_chunk(1)
+        quantise(1)
+        take_smaller(3)
         give_sign(2)
-        score_chunk(2)
+        give_sign(3)
+        quantise(2)
+        quantise(3)
+        for t in range(1, PACK):
+            multiply(t, 0, S)
 
         out_rows = out.rearrange("(p t) w -> p t w", t=PACK)
         for t in range(PACK):
-            score = sb(f"score{t}", [P, S], F32, tag=("score_even", "score_odd")[t % 2])
-            positive = sb(f"positive{t}", [P, S], F32, tag="positive")
-            pull = sb(f"pull{t}", [P, S], F32)
-            spans = CHUNKS if t == 0 else ((0, S),)
-            for lo, hi in spans[:-1]:
-                nc.scalar.activation(positive[:, lo:hi], s_out(t, lo, hi), ACT.Relu, scale=SIXTEENTH)
-                nc.scalar.activation(score[:, lo:hi], s_out(t, lo, hi), ACT.Copy, scale=SIXTEENTH)
-            lo, hi = spans[-1]
-            nc.scalar.activation(positive[:, lo:hi], s_out(t, lo, hi), ACT.Relu, scale=SIXTEENTH)
+            score = sbuf(f"score{t}", [P, S], F32, tag=("score_even", "score_odd")[t % 2])
+            positive = sbuf(f"positive{t}", [P, S], F32, tag="positive")
+            pull = sbuf(f"pull{t}", [P, S], F32)
+            ranges = SPANS if t == 0 else ((0, S),)
+            early, late = ranges[:-2], ranges[-2:]
+            for lo, hi in early:
+                nc.scalar.activation(positive[:, lo:hi], s_sums(t, lo, hi), ACT.Relu, scale=SIXTEENTH)
+                nc.scalar.activation(score[:, lo:hi], s_sums(t, lo, hi), ACT.Copy, scale=SIXTEENTH)
+            for lo, hi in late:
+                nc.scalar.activation(positive[:, lo:hi], s_sums(t, lo, hi), ACT.Relu, scale=SIXTEENTH)
             if t == 0:
-                nc.scalar.activation(pull[:, 0:128], positive[:].indirect(entries(n4_t, 0, 128)), ACT.Copy, scale=-1.0)
+                nc.scalar.activation(
+                    pull[:, 0:QUARTER], positive[:].indirect(entries(n4_list, 0, QUARTER)), ACT.Copy, scale=-1.0
+                )
                 nc.vector.tensor_scalar(
-                    pull[:, 128:256], positive[:].indirect(entries(n4_t, 128, 256)), -1.0, 0.0, ALU.mult, ALU.add
+                    pull[:, QUARTER:HALF],
+                    positive[:].indirect(entries(n4_list, QUARTER, HALF)),
+                    -1.0,
+                    0.0,
+                    ALU.mult,
+                    ALU.add,
                 )
             else:
-                nc.scalar.activation(pull[:, 0:256], positive[:].indirect(entries(n4_t, 0, 256)), ACT.Copy, scale=-1.0)
-            nc.scalar.activation(score[:, lo:hi], s_out(t, lo, hi), ACT.Copy, scale=SIXTEENTH)
-            nc.scalar.activation(pull[:, 256:S], positive[:].indirect(entries(n4_t, 256, S)), ACT.Copy, scale=-1.0)
-            pieces = HALVES if t == 0 else ((0, S),)
-            for lo, hi in pieces:
+                nc.scalar.activation(
+                    pull[:, 0:HALF], positive[:].indirect(entries(n4_list, 0, HALF)), ACT.Copy, scale=-1.0
+                )
+            for lo, hi in late:
+                nc.scalar.activation(score[:, lo:hi], s_sums(t, lo, hi), ACT.Copy, scale=SIXTEENTH)
+            nc.scalar.activation(pull[:, HALF:S], positive[:].indirect(entries(n4_list, HALF, S)), ACT.Copy, scale=-1.0)
+            for lo, hi in HALVES if t == 0 else ((0, S),):
                 nc.vector.tensor_tensor(
-                    pages[t][:].indirect(entries(n3_t, lo, hi)), score[:, lo:hi], pull[:, lo:hi], ALU.add
+                    pages[t][:].indirect(entries(n3_list, lo, hi)), score[:, lo:hi], pull[:, lo:hi], ALU.add
                 )
             nc.sync.dma_start(out_rows[:, t, :], pages[t][:])

from contextlib import ExitStack

import concourse.mybir as mybir

K, T, S, G, H, C, U = 512, 1024, 512, 2048, 512, 512, 1024
FLOPS = 2 * K * H * S + 2 * K * C * S

F32 = mybir.dt.float32
BF16 = mybir.dt.bfloat16
I32 = mybir.dt.int32
U32 = mybir.dt.uint32
U16 = mybir.dt.uint16
U8 = mybir.dt.uint8
FP8X4 = mybir.dt.float8_e4m3fn_x4
ALU = mybir.AluOpType
ACT = mybir.ActivationFunctionType

P = 128
PACK = 4
GROUP = 16
SIXTEENTH = 0.0625
HALF, QUARTER = S // 2, S // 4

HALVES = ((0, HALF), (HALF, S))
CHUNKS = ((0, HALF), (HALF, HALF + QUARTER), (HALF + QUARTER, S))
SPANS = ((0, 256), (256, 384), (384, 448), (448, 512))
VECTOR_N2 = ((0, 0), (0, 1), (0, 2), (0, 3), (1, 0))


def entries(offsets, lo, hi):
    return offsets[:, lo // GROUP : hi // GROUP]


def tile_picked_pqcminmxpagez_none_p_kernel(
    tc, x_words, x_scales, d_words, d_scales, gs, offs, k1, n1, n2, cand, n3, n4, out
):
    nc = tc.nc
    with ExitStack() as ctx:
        keep = ctx.enter_context(tc.tile_pool(name="keep", bufs=1))
        shared = ctx.enter_context(tc.tile_pool(name="shared", bufs=1))
        psum = ctx.enter_context(tc.psum_pool(name="psum", bufs=1))

        def sbuf(name, shape, dtype, tag=None):
            return keep.tile(shape, dtype, name=name, tag=tag or name, align_bytes=64)

        def load_list(name, source):
            tile = sbuf(name, [P, S // GROUP], U16)
            nc.sync.dma_start(tile[:], source)
            return tile

        d_byte_table = sbuf("d_byte_table", [P, G], U8)
        x_byte_table = sbuf("x_byte_table", [P, T], U8)
        d_plane = sbuf("d_plane", [P, H], U8)
        nc.vector.memset(d_byte_table[:].bitcast(I32), 0)
        nc.vector.memset(x_byte_table[:].bitcast(I32), 0)
        nc.vector.memset(d_plane[:].bitcast(I32), 0)

        k1_list = load_list("k1_list", k1)
        offs_list = load_list("offs_list", offs)
        nc.sync.dma_start(d_byte_table[0:P:8, :].bitcast(I32), d_scales[0].bitcast(I32))
        d_word_table = sbuf("d_word_table", [P, G], U32)
        nc.sync.dma_start(d_word_table[:].bitcast(I32), d_words[0].rearrange("p n j -> p (n j)").bitcast(I32))
        for q in range(PACK):
            nc.sync.dma_start(
                x_byte_table[32 * q : 32 * q + 4, :].bitcast(I32), x_scales[0, 4 * q : 4 * q + 4, :].bitcast(I32)
            )
        x_word_table = sbuf("x_word_table", [P, T], U32)
        nc.sync.dma_start(x_word_table[:].bitcast(I32), x_words[0].rearrange("p n j -> p (n j)").bitcast(I32))
        gain = sbuf("gain", [P, PACK], F32)
        nc.sync.dma_start(gain[:], gs.rearrange("(p t) o -> p (t o)", t=PACK))

        pages = [sbuf(f"page{t}", [P, U], F32) for t in range(PACK)]
        nc.vector.memset(pages[0][:], 0.0)
        for t in range(1, PACK):
            nc.scalar.copy(pages[t][:], pages[0][:])

        gain_size = sbuf("gain_size", [P, PACK], F32)
        gain_sign = sbuf("gain_sign", [P, HALF, PACK], BF16)
        nc.scalar.activation(gain_size[:], gain[:], ACT.Abs, scale=SIXTEENTH)
        nc.scalar.activation(gain_sign[:], gain[:].unsqueeze(1).to_broadcast([P, HALF, PACK]), ACT.Sign)

        word_bytes = 4 * H
        d_bytes_picked = shared.tile([P, H], U8, name="d_bytes_picked", align_bytes=64, offset=word_bytes - H // 2)
        d_bytes_dealt = shared.tile([P, H], U8, name="d_bytes_dealt", align_bytes=64, offset=word_bytes + HALF)
        token_plane = [
            shared.tile([P, HALF], U8, name=f"token_plane{half}", align_bytes=64, offset=word_bytes + HALF * half)
            for half in range(2)
        ]
        d_words_picked = shared.tile([P, H], U32, name="d_words_picked", align_bytes=64, offset=0)
        d_codes = sbuf("d_codes", [P, H], U32)

        nc.vector.tensor_copy(d_bytes_picked[:], d_byte_table[:].indirect(k1_list[:]))
        nc.vector.tensor_copy(
            d_bytes_dealt[:].rearrange("p (t a i) -> p a t i", t=PACK, i=16),
            d_bytes_picked[:].rearrange("p (a i t) -> p a t i", t=PACK, i=16),
        )
        for q in range(PACK):
            nc.sync.dma_start(
                d_plane[32 * q : 32 * q + 4, :].bitcast(I32), d_bytes_dealt[32 * q : 32 * q + 32 : 8, :].bitcast(I32)
            )
        cand_list = load_list("cand_list", cand)
        n1_list = load_list("n1_list", n1)
        n2_list = load_list("n2_list", n2)
        n4_list = load_list("n4_list", n4)
        n3_list = load_list("n3_list", n3)
        nc.vector.tensor_copy(d_words_picked[:], d_word_table[:].indirect(k1_list[:]))
        nc.vector.tensor_copy(token_plane[0][:], x_byte_table[:].indirect(entries(offs_list, 0, HALF)))
        nc.vector.tensor_copy(
            d_codes[:].rearrange("p (t a i) -> p a t i", t=PACK, i=4),
            d_words_picked[:].rearrange("p (a i t) -> p a t i", t=PACK, i=4),
        )

        u = [sbuf(f"u{t}", [P, S], F32) for t in range(PACK)]
        for half, (lo, hi) in enumerate(HALVES):
            token_codes = sbuf(f"token_codes{half}", [P, hi - lo], U32)
            if half == 1:
                nc.vector.tensor_copy(token_plane[1][:], x_byte_table[:].indirect(entries(offs_list, lo, hi)))
            nc.vector.tensor_copy(token_codes[:], x_word_table[:].indirect(entries(offs_list, lo, hi)))
            for pair in range(2):
                bank = psum.tile([P, 2, hi - lo], F32, name=f"h_bank{half}{pair}", tag=f"h_bank{half}{pair}")
                for slot in range(2):
                    t = 2 * pair + slot
                    nc.tensor.matmul_mx(
                        out=bank[:, slot, :],
                        lhsT=d_codes[:, P * t : P * (t + 1)].bitcast(FP8X4),
                        lhsT_scale=d_plane[:, P * t : P * (t + 1)],
                        rhs=token_codes[:].bitcast(FP8X4),
                        rhs_scale=token_plane[half][:],
                        start=True,
                        stop=True,
                    )
                for slot in range(2):
                    t = 2 * pair + slot
                    nc.scalar.activation(u[t][:, lo:hi], bank[:, slot, :], ACT.Copy, scale=gain_size[:, t : t + 1])

        cand_codes = sbuf("cand_codes", [P, C], U32)
        cand_plane = sbuf("cand_plane", [P, C], U8)
        nc.vector.tensor_copy(
            cand_codes[:].rearrange("p (t m) -> p m t", t=PACK), x_word_table[:].indirect(cand_list[:])
        )
        nc.vector.tensor_copy(
            cand_plane[:].rearrange("p (t m) -> p m t", t=PACK), x_byte_table[:].indirect(cand_list[:])
        )

        first = [sbuf(f"first{half}", [P, PACK, hi - lo], F32) for half, (lo, hi) in enumerate(HALVES)]
        larger = [sbuf(f"larger{half}", [P, PACK, hi - lo], F32) for half, (lo, hi) in enumerate(HALVES)]
        second = [sbuf(f"second{chunk}", [P, PACK, hi - lo], F32) for chunk, (lo, hi) in enumerate(CHUNKS)]
        z_unsigned = [sbuf(f"z_unsigned{span}", [P, hi - lo, PACK], BF16) for span, (lo, hi) in enumerate(SPANS)]
        z = [
            sbuf(f"z{span}", [P, hi - lo, PACK], BF16, tag="score_odd" if span == len(SPANS) - 1 else None)
            for span, (lo, hi) in enumerate(SPANS)
        ]
        z_codes = sbuf("z_codes", [P, S], U32)
        z_plane = sbuf("z_plane", [P, S], U8)
        lead_tags = ("lead0", "lead1", "lead2", "h_bank10")
        lead_bank = [
            psum.tile([P, hi - lo], F32, name=f"lead_bank{span}", tag=lead_tags[span])
            for span, (lo, hi) in enumerate(SPANS)
        ]
        later_tags = {1: "s_bank1", 2: "h_bank00", 3: "h_bank01"}
        later_bank = {t: psum.tile([P, S], F32, name=f"s_bank{t}", tag=later_tags[t]) for t in range(1, PACK)}

        def s_sums(t, lo, hi):
            if t > 0:
                return later_bank[t][:, lo:hi]
            return lead_bank[SPANS.index((lo, hi))][:]

        def fetch_first(half):
            lo, hi = HALVES[half]
            for t in range(PACK):
                nc.scalar.activation(first[half][:, t, :], u[t][:].indirect(entries(n1_list, lo, hi)), ACT.Copy)

        def fetch_second(chunk):
            lo, hi = CHUNKS[chunk]
            for t in range(PACK):
                if (chunk, t) in VECTOR_N2:
                    nc.vector.tensor_copy(second[chunk][:, t, :], u[t][:].indirect(entries(n2_list, lo, hi)))
                else:
                    nc.scalar.activation(second[chunk][:, t, :], u[t][:].indirect(entries(n2_list, lo, hi)), ACT.Copy)

        def take_larger(half, t):
            lo, hi = HALVES[half]
            nc.vector.tensor_tensor(larger[half][:, t, :], u[t][:, lo:hi], first[half][:, t, :], ALU.max)

        def take_smaller(span):
            lo, hi = SPANS[span]
            half, chunk = lo // HALF, min(span, len(CHUNKS) - 1)
            half_lo, chunk_lo = HALVES[half][0], CHUNKS[chunk][0]
            nc.vector.tensor_tensor(
                z_unsigned[span][:].rearrange("p (c i) t -> p c t i", i=4),
                larger[half][:, :, lo - half_lo : hi - half_lo].rearrange("p t (c i) -> p c t i", i=4),
                second[chunk][:, :, lo - chunk_lo : hi - chunk_lo].rearrange("p t (c i) -> p c t i", i=4),
                ALU.min,
            )

        def give_sign(span):
            lo, hi = SPANS[span]
            nc.vector.tensor_tensor(z[span][:], z_unsigned[span][:], gain_sign[:, 0 : hi - lo, :], ALU.mult)

        def multiply(t, lo, hi):
            nc.tensor.matmul_mx(
                out=s_sums(t, lo, hi),
                lhsT=cand_codes[:, P * t : P * (t + 1)].bitcast(FP8X4),
                lhsT_scale=cand_plane[:, P * t : P * (t + 1)],
                rhs=z_codes[:, lo:hi].bitcast(FP8X4),
                rhs_scale=z_plane[:, lo:hi],
                start=True,
                stop=True,
            )

        def quantise(span):
            lo, hi = SPANS[span]
            nc.vector.quantize_mx(
                out=z_codes[:, lo:hi].bitcast(FP8X4),
                scales=z_plane[:, lo:hi],
                in_=z[span][:].rearrange("p c t -> p (c t)"),
            )
            multiply(0, lo, hi)

        fetch_first(0)
        fetch_second(0)
        fetch_first(1)
        fetch_second(1)
        fetch_second(2)
        for t in range(PACK):
            take_larger(0, t)
        take_larger(1, 0)
        take_smaller(0)
        take_larger(1, 1)
        give_sign(0)
        take_larger(1, 2)
        quantise(0)
        take_larger(1, 3)
        take_smaller(1)
        give_sign(1)
        take_smaller(2)
        quantise(1)
        take_smaller(3)
        give_sign(2)
        give_sign(3)
        quantise(2)
        quantise(3)
        for t in range(1, PACK):
            multiply(t, 0, S)

        out_rows = out.rearrange("(p t) w -> p t w", t=PACK)
        for t in range(PACK):
            score = sbuf(f"score{t}", [P, S], F32, tag=("score_even", "score_odd")[t % 2])
            positive = sbuf(f"positive{t}", [P, S], F32, tag="positive")
            pull = sbuf(f"pull{t}", [P, S], F32)
            ranges = SPANS if t == 0 else ((0, S),)
            early, late = ranges[:-2], ranges[-2:]
            for lo, hi in early:
                nc.scalar.activation(positive[:, lo:hi], s_sums(t, lo, hi), ACT.Relu, scale=SIXTEENTH)
                nc.scalar.activation(score[:, lo:hi], s_sums(t, lo, hi), ACT.Copy, scale=SIXTEENTH)
            for lo, hi in late:
                nc.scalar.activation(positive[:, lo:hi], s_sums(t, lo, hi), ACT.Relu, scale=SIXTEENTH)
            if t == 0:
                nc.scalar.activation(
                    pull[:, 0:QUARTER], positive[:].indirect(entries(n4_list, 0, QUARTER)), ACT.Copy, scale=-1.0
                )
                nc.vector.tensor_scalar(
                    pull[:, QUARTER:HALF],
                    positive[:].indirect(entries(n4_list, QUARTER, HALF)),
                    -1.0,
                    0.0,
                    ALU.mult,
                    ALU.add,
                )
            else:
                nc.scalar.activation(
                    pull[:, 0:HALF], positive[:].indirect(entries(n4_list, 0, HALF)), ACT.Copy, scale=-1.0
                )
            for lo, hi in late:
                nc.scalar.activation(score[:, lo:hi], s_sums(t, lo, hi), ACT.Copy, scale=SIXTEENTH)
            nc.scalar.activation(pull[:, HALF:S], positive[:].indirect(entries(n4_list, HALF, S)), ACT.Copy, scale=-1.0)
            for lo, hi in HALVES if t == 0 else ((0, S),):
                nc.vector.tensor_tensor(
                    pages[t][:].indirect(entries(n3_list, lo, hi)), score[:, lo:hi], pull[:, lo:hi], ALU.add
                )
            nc.sync.dma_start(out_rows[:, t, :], pages[t][:])
